import numpy as np
import ml_dtypes


def mxq(x, axis, fmt="e4m3"):
    dtype, down = {"e4m3": (ml_dtypes.float8_e4m3fn, 7), "e5m2": (ml_dtypes.float8_e5m2, 14)}[fmt]
    v = np.moveaxis(np.asarray(x, np.float32).astype(ml_dtypes.bfloat16).astype(np.float64), axis, -1)
    blocks = v.reshape(v.shape[:-1] + (-1, 32))
    amax = np.abs(blocks).max(-1, keepdims=True)
    byte = np.maximum(np.where(amax > 0, np.frexp(amax)[1] - 1 + 127, 0) - down, 1)
    scale = np.exp2(byte - 127.0)
    codes = (blocks / scale).astype(np.float32).astype(dtype).astype(np.float64)
    return np.moveaxis((codes * scale).reshape(v.shape), -1, axis)


WIDE = False


def mx_kscale(k):
    if not WIDE:
        return np.ones(k)
    levels = np.array([10, -10, 5, -5, 0])
    if k % 512:
        return np.exp2(np.random.permutation(np.resize(levels, k // 32))).repeat(32)
    a = np.empty((k // 512, 16))
    for p in range(k // 512):
        a[p, :8] = np.random.permutation(np.resize(levels, 8))
        for g in range(8):
            far = levels[np.abs(levels - a[p, g]) >= 10]
            a[p, g + 8] = far[np.random.randint(len(far))]
    return np.exp2(a.ravel()).repeat(32)


def f64(x):
    return np.asarray(x).astype(np.float64)


def striped(idx):
    return np.tile(np.asarray(idx).reshape(-1, 16).T, (8, 1)).astype(np.uint16)


def unstriped(offs):
    return offs[:16].T.reshape(-1).astype(np.int64)


E2M1 = np.array([0.0, 0.5, 1.0, 1.5, 2.0, 3.0, 4.0, 6.0, -0.0, -0.5, -1.0, -1.5, -2.0, -3.0, -4.0, -6.0])


def pack_weight(w, fmt):
    k, n = w.shape
    w = f64(np.asarray(w, np.float32).astype(ml_dtypes.bfloat16)).reshape(k // 32, 32, n)
    amax = np.abs(w).max(1)
    if fmt == "e4m3":
        byte = np.frexp(amax)[1] - 1 + 127 - 7
    else:
        mant, ex = np.frexp(amax / 6.0)
        byte = np.where(mant > 0.5, ex, ex - 1) + 127
    byte = np.clip(np.where(amax > 0, byte, 1), 1, 254)
    scaled = (w * np.exp2(127.0 - byte)[:, None, :]).reshape(k, n).astype(np.float32)
    by_word = np.ascontiguousarray(scaled.reshape(k // 512, 128, 4, n).transpose(0, 1, 3, 2))
    if fmt == "e4m3":
        words = by_word.astype(ml_dtypes.float8_e4m3fn).view(np.uint8)
    else:
        c = by_word.astype(ml_dtypes.float4_e2m1fn).view(np.uint8) & 0xF
        words = (c[..., 0::2] | (c[..., 1::2] << 4)).reshape(k // 512, 128, 2 * n)
    return np.ascontiguousarray(words), np.ascontiguousarray(byte.astype(np.uint8).reshape(k // 512, 16, n))


def unpack_weight(words, scales, fmt):
    g, _, n = scales.shape
    words = np.ascontiguousarray(words).reshape(g, 128, n, -1)
    if fmt == "e4m3":
        vals = words.view(ml_dtypes.float8_e4m3fn).astype(np.float64)
    else:
        nib = np.empty((g, 128, n, 4), np.uint8)
        nib[..., 0::2] = words & 0xF
        nib[..., 1::2] = words >> 4
        vals = E2M1[nib]
    vals = vals * np.repeat(np.exp2(scales.astype(np.float64) - 127.0), 8, axis=1)[..., None]
    return vals.transpose(0, 1, 3, 2).reshape(g * 512, n)


D, E, T, I, Q = 512, 512, 2048, 512, 128


def setup_inputs():
    n = np.random.standard_normal
    idx2 = np.random.permutation(I)[:I]
    idx = np.random.permutation(T)[:I]
    fd = mx_kscale(D)
    fi = mx_kscale(I)
    ti = np.ones(T)
    ti[idx] = fi
    keysp = pack_weight(n((D, T)) / fd[:, None], "e2m1")
    return {
        "query": (n((D, Q)) * 0.8 / np.sqrt(D) * fd[:, None]).astype(np.float32),
        "keys_words": keysp[0],
        "keys_scales": keysp[1],
        "reserve": (np.random.uniform(0.5, 2.0, (Q, 1))).astype(np.float32),
        "os": (np.random.uniform(4.0, 16.0, (1, I)) * fi).astype(np.float32),
        "vals": (n((E, T)) / ti).astype(np.float32),
        "offs2": striped(idx2),
        "offs": striped(idx),
    }


def reference(query, keys_words, keys_scales, reserve, os, vals, offs2, offs):
    idx2 = unstriped(offs2)
    idx = unstriped(offs)
    keysu = unpack_weight(keys_words, keys_scales, "e2m1")
    queryq = mxq(f64(query), 0, "e4m3")
    keysidxg = keysu[:, idx]
    a = queryq.T @ keysidxg
    p = np.exp(a)
    z = np.sum(p, axis=1, keepdims=True)
    r = p / (p + p[:, idx2] + f64(reserve))
    w = p / z * r
    wo1 = w * f64(os)
    wt1 = wo1.T
    vt1 = f64(vals)[:, idx].T
    wt1q = mxq(wt1, 0, "e4m3")
    vt1q = mxq(vt1, 0, "e4m3")
    o = wt1q.T @ vt1q
    return o

@@ -1,0 +1,169 @@
+from contextlib import ExitStack
+
+import concourse.mybir as mybir
+from concourse.masks import make_identity
+
+D, E, T, I, Q = 512, 512, 2048, 512, 128
+FLOPS = 2 * Q * I * D + 2 * Q * I * E
+
+F32 = mybir.dt.float32
+BF16 = mybir.dt.bfloat16
+I32 = mybir.dt.int32
+U32 = mybir.dt.uint32
+U16 = mybir.dt.uint16
+U8 = mybir.dt.uint8
+FP8X4 = mybir.dt.float8_e4m3fn_x4
+FP4X4 = mybir.dt.float4_e2m1fn_x4
+ACT = mybir.ActivationFunctionType
+ALU = mybir.AluOpType
+
+P = 128
+PACK = 4
+BLOCKS = E // P
+P_WINDOW = 704
+TINY = 2.0 ** -100
+
+
+def turn_and_quantise(nc, psum, sb, ident, rows_bf16, tag, bank):
+    words = rows_bf16[:].bitcast(F32)
+    turned = psum.tile([P, 2, P], F32, name="turned_" + bank)
+    for u in range(2):
+        nc.tensor.transpose(turned[:, u, :], words[:, u::2], ident[:])
+    grouped = sb.tile([P, P * PACK], BF16, align_bytes=64, name="grouped_" + tag)
+    nc.scalar.copy(
+        out=grouped[:].bitcast(F32).rearrange("s (c u) -> s c u", u=2),
+        in_=turned[:].rearrange("s u c -> s c u"),
+    )
+    codes = sb.tile([P, P], U32, align_bytes=64, name="codes_" + tag)
+    scales = sb.tile([P, P], U8, align_bytes=64, name="scales_" + tag)
+    nc.vector.quantize_mx(out=codes[:].bitcast(FP8X4), scales=scales[:], in_=grouped[:])
+    return codes, scales
+
+
+def tile_attend_neighbourshare_kernel(tc, query, keys_words, keys_scales, reserve, slot_factor, vals, offs2, offs, out):
+    nc = tc.nc
+    with ExitStack() as ctx:
+        sb = ctx.enter_context(tc.tile_pool(name="sb", bufs=1))
+        psum = ctx.enter_context(tc.psum_pool(name="psum", bufs=1))
+
+        slots = sb.tile([P, I // 16], U16, name="slots")
+        nc.sync.dma_start(slots[:], offs)
+        key_words = sb.tile([P, T], U16, name="key_words")
+        nc.sync.dma_start(key_words[:].bitcast(I32), keys_words[0].bitcast(I32))
+        q_raw = sb.tile([P, PACK, Q], F32, name="q_raw")
+        nc.sync.dma_start(q_raw[:], query.rearrange("(p j) q -> p j q", j=PACK))
+
+        key_scales = sb.tile([P, T], U8, name="key_scales")
+        nc.vector.memset(key_scales[:].bitcast(I32), 0)
+        for quad in range(4):
+            nc.scalar.dma_start(
+                key_scales[32 * quad : 32 * quad + 4, :].bitcast(I32),
+                keys_scales[0, 4 * quad : 4 * quad + 4, :].bitcast(I32),
+            )
+
+        pools = [sb.tile([P, T], F32, name="val_pool0")]
+        nc.sync.dma_start(pools[0][:], vals[0:P, :])
+        links = sb.tile([P, I // 16], U16, name="links")
+        nc.sync.dma_start(links[:], offs2)
+
+        reserve_col = sb.tile([P, 1], F32, name="reserve_col")
+        nc.gpsimd.dma_start(reserve_col[:], reserve)
+        os_cols = sb.tile([P, PACK], F32, name="os_cols")
+        nc.gpsimd.dma_start(os_cols[:], slot_factor.rearrange("o (s t) -> (o s) t", t=PACK))
+        ident = sb.tile([P, P], F32, name="ident")
+        make_identity(nc, ident[:])
+
+        p = sb.tile([P, P_WINDOW], F32, name="p")
+        nc.vector.memset(p[:, I:], 0.0)
+
+        q_grouped = sb.tile([P, Q, PACK], BF16, align_bytes=64, name="q_grouped")
+        nc.scalar.activation(out=q_grouped[:], in_=q_raw[:].rearrange("p j q -> p q j"), func=ACT.Copy)
+        k_words = sb.tile([P, I], U16, align_bytes=64, name="k_words")
+        nc.vector.tensor_copy(k_words[:], key_words[:].indirect(slots[:]))
+        k_scales = sb.tile([P, I], U8, align_bytes=64, name="k_scales")
+        nc.vector.tensor_copy(k_scales[:], key_scales[:].indirect(slots[:]))
+        q_codes = sb.tile([P, Q], U32, align_bytes=64, name="q_codes")
+        q_scales = sb.tile([P, Q], U8, align_bytes=64, name="q_scales")
+        nc.vector.quantize_mx(
+            out=q_codes[:].bitcast(FP8X4), scales=q_scales[:], in_=q_grouped[:].rearrange("p q j -> p (q j)")
+        )
+
+        for b, tag in ((1, "key_words"), (2, "q_raw"), (3, "key_scales")):
+            pools.append(sb.tile([P, T], F32, name="val_pool%d" % b, tag=tag))
+            nc.sync.dma_start(pools[b][:], vals[b * P : (b + 1) * P, :])
+
+        scores = psum.tile([P, I], F32, name="scores")
+        nc.tensor.matmul_mx(
+            out=scores[:],
+            lhsT=q_codes[:].bitcast(FP8X4),
+            lhsT_scale=q_scales[:],
+            rhs=k_words[:].bitcast(FP4X4),
+            rhs_scale=k_scales[:],
+            start=True,
+            stop=True,
+        )
+
+        os_bank = psum.tile([P, PACK, P], F32, name="os_bank")
+        for t in range(PACK):
+            nc.tensor.transpose(os_bank[:, t, :], os_cols[:, t : t + 1].to_broadcast([P, P]), ident[:])
+
+        def gather_values(b, tag):
+            picked = sb.tile([P, I], BF16, align_bytes=64, name="picked%d" % b, tag=tag)
+            nc.vector.tensor_copy(picked[:], pools[b][:].indirect(slots[:]))
+            return picked
+
+        neg_max = sb.tile([P, 1], F32, name="neg_max")
+        nc.vector.tensor_reduce(neg_max[:], scores[:], axis=mybir.AxisListType.X, op=ALU.max, negate=True)
+        shrink = sb.tile([P, 1], F32, name="shrink")
+        nc.scalar.activation(out=shrink[:], in_=neg_max[:], func=ACT.Exp)
+        z = sb.tile([P, 1], F32, name="z")
+        nc.scalar.activation(out=p[:, :I], in_=scores[:], func=ACT.Exp, bias=neg_max[:], accum_out=z[:])
+        rest = sb.tile([P, 1], F32, name="rest")
+        nc.scalar.activation(out=rest[:], in_=shrink[:], func=ACT.Identity, scale=reserve_col[:], bias=TINY)
+        z_root = sb.tile([P, 1], F32, name="z_root")
+        nc.scalar.activation(out=z_root[:], in_=z[:], func=ACT.Abs_reciprocal_sqrt)
+        share = sb.tile([P, I], F32, align_bytes=64, name="share")
+        nc.scalar.activation(out=share[:], in_=p[:, :I], func=ACT.Square, scale=z_root[:])
+
+        picked0 = gather_values(0, "k_words")
+
+        linked = sb.tile([P, I], F32, align_bytes=64, name="linked")
+        nc.vector.tensor_copy(linked[:], p[:].indirect(links[:]))
+        pair = sb.tile([P, I], F32, name="pair")
+        nc.vector.tensor_tensor(pair[:], linked[:], p[:, :I], ALU.add)
+        root = sb.tile([P, I], F32, name="root")
+        nc.scalar.activation(out=root[:], in_=pair[:], func=ACT.Abs_reciprocal_sqrt, bias=rest[:])
+        inv = sb.tile([P, I], F32, align_bytes=64, name="inv")
+        nc.scalar.activation(out=inv[:], in_=root[:], func=ACT.Square)
+        picked1 = gather_values(1, "linked")
+        top = sb.tile([P, I], F32, name="top")
+        nc.vector.tensor_tensor(
+            top[:].rearrange("q (s t) -> q s t", t=PACK),
+            share[:].rearrange("q (s t) -> q s t", t=PACK),
+            os_bank[:].rearrange("q t s -> q s t"),
+            ALU.mult,
+        )
+        vq = [turn_and_quantise(nc, psum, sb, ident, picked0, "v0", "a")]
+        picked2 = gather_values(2, "share")
+        w = sb.tile([P, I], BF16, name="w")
+        nc.vector.tensor_tensor(w[:], top[:], inv[:], ALU.mult)
+        picked3 = gather_values(3, "inv")
+        vq.append(turn_and_quantise(nc, psum, sb, ident, picked1, "v1", "b"))
+        w_codes, w_scales = turn_and_quantise(nc, psum, sb, ident, w, "w", "w")
+        vq.append(turn_and_quantise(nc, psum, sb, ident, picked2, "v2", "a"))
+        vq.append(turn_and_quantise(nc, psum, sb, ident, picked3, "v3", "b"))
+
+        for b in range(BLOCKS):
+            acc = psum.tile([P, P], F32, name="acc%d" % (b % 2))
+            nc.tensor.matmul_mx(
+                out=acc[:],
+                lhsT=w_codes[:].bitcast(FP8X4),
+                lhsT_scale=w_scales[:],
+                rhs=vq[b][0][:].bitcast(FP8X4),
+                rhs_scale=vq[b][1][:],
+                start=True,
+                stop=True,
+            )
+            res = sb.tile([P, P], F32, name="res%d" % b)
+            nc.scalar.copy(out=res[:], in_=acc[:])
+            nc.sync.dma_start(out[:, b * P : (b + 1) * P], res[:])

@@ -21,23 +21,20 @@ P = 128
 PACK = 4
 BLOCKS = E // P
 P_WINDOW = 704
+CLEAR_SPLIT = 1408
+HALF = I // 2
 TINY = 2.0 ** -100
 
 
-def turn_and_quantise(nc, psum, sb, ident, rows_bf16, tag, bank):
+def turn(nc, psum, ident, rows_bf16, grouped, bank):
     words = rows_bf16[:].bitcast(F32)
     turned = psum.tile([P, 2, P], F32, name="turned_" + bank)
     for u in range(2):
         nc.tensor.transpose(turned[:, u, :], words[:, u::2], ident[:])
-    grouped = sb.tile([P, P * PACK], BF16, align_bytes=64, name="grouped_" + tag)
     nc.scalar.copy(
-        out=grouped[:].bitcast(F32).rearrange("s (c u) -> s c u", u=2),
+        out=grouped.bitcast(F32).rearrange("s (c u) -> s c u", u=2),
         in_=turned[:].rearrange("s u c -> s c u"),
     )
-    codes = sb.tile([P, P], U32, align_bytes=64, name="codes_" + tag)
-    scales = sb.tile([P, P], U8, align_bytes=64, name="scales_" + tag)
-    nc.vector.quantize_mx(out=codes[:].bitcast(FP8X4), scales=scales[:], in_=grouped[:])
-    return codes, scales
 
 
 def tile_attend_neighbourshare_kernel(tc, query, keys_words, keys_scales, reserve, slot_factor, vals, offs2, offs, out):
@@ -46,30 +43,32 @@ def tile_attend_neighbourshare_kernel(tc, query, keys_words, keys_scales, reserv
         sb = ctx.enter_context(tc.tile_pool(name="sb", bufs=1))
         psum = ctx.enter_context(tc.psum_pool(name="psum", bufs=1))
 
+        key_scales = sb.tile([P, T], U8, name="key_scales")
+        nc.vector.memset(key_scales[:, :CLEAR_SPLIT].bitcast(I32), 0)
+        nc.gpsimd.memset(key_scales[:, CLEAR_SPLIT:].bitcast(I32), 0)
+
         slots = sb.tile([P, I // 16], U16, name="slots")
         nc.sync.dma_start(slots[:], offs)
         key_words = sb.tile([P, T], U16, name="key_words")
         nc.sync.dma_start(key_words[:].bitcast(I32), keys_words[0].bitcast(I32))
-        q_raw = sb.tile([P, PACK, Q], F32, name="q_raw")
-        nc.sync.dma_start(q_raw[:], query.rearrange("(p j) q -> p j q", j=PACK))
-
-        key_scales = sb.tile([P, T], U8, name="key_scales")
-        nc.vector.memset(key_scales[:].bitcast(I32), 0)
         for quad in range(4):
-            nc.scalar.dma_start(
+            nc.sync.dma_start(
                 key_scales[32 * quad : 32 * quad + 4, :].bitcast(I32),
                 keys_scales[0, 4 * quad : 4 * quad + 4, :].bitcast(I32),
             )
-
-        pools = [sb.tile([P, T], F32, name="val_pool0")]
+        q_raw = sb.tile([P, PACK, Q], F32, name="q_raw")
+        nc.sync.dma_start(q_raw[:], query.rearrange("(p j) q -> p j q", j=PACK))
+        os_cols = sb.tile([P, PACK], F32, name="os_cols")
+        nc.sync.dma_start(os_cols[:], slot_factor.rearrange("o (s t) -> (o s) t", t=PACK))
+        pools = [sb.tile([P, T], F32, align_bytes=64, name="val_pool%d" % b) for b in range(BLOCKS)]
         nc.sync.dma_start(pools[0][:], vals[0:P, :])
         links = sb.tile([P, I // 16], U16, name="links")
         nc.sync.dma_start(links[:], offs2)
-
         reserve_col = sb.tile([P, 1], F32, name="reserve_col")
-        nc.gpsimd.dma_start(reserve_col[:], reserve)
-        os_cols = sb.tile([P, PACK], F32, name="os_cols")
-        nc.gpsimd.dma_start(os_cols[:], slot_factor.rearrange("o (s t) -> (o s) t", t=PACK))
+        nc.sync.dma_start(reserve_col[:], reserve)
+        for b in range(1, BLOCKS):
+            nc.sync.dma_start(pools[b][:], vals[b * P : (b + 1) * P, :])
+
         ident = sb.tile([P, P], F32, name="ident")
         make_identity(nc, ident[:])
 
@@ -78,92 +77,106 @@ def tile_attend_neighbourshare_kernel(tc, query, keys_words, keys_scales, reserv
 
         q_grouped = sb.tile([P, Q, PACK], BF16, align_bytes=64, name="q_grouped")
         nc.scalar.activation(out=q_grouped[:], in_=q_raw[:].rearrange("p j q -> p q j"), func=ACT.Copy)
-        k_words = sb.tile([P, I], U16, align_bytes=64, name="k_words")
-        nc.vector.tensor_copy(k_words[:], key_words[:].indirect(slots[:]))
-        k_scales = sb.tile([P, I], U8, align_bytes=64, name="k_scales")
-        nc.vector.tensor_copy(k_scales[:], key_scales[:].indirect(slots[:]))
         q_codes = sb.tile([P, Q], U32, align_bytes=64, name="q_codes")
         q_scales = sb.tile([P, Q], U8, align_bytes=64, name="q_scales")
         nc.vector.quantize_mx(
             out=q_codes[:].bitcast(FP8X4), scales=q_scales[:], in_=q_grouped[:].rearrange("p q j -> p (q j)")
         )
 
-        for b, tag in ((1, "key_words"), (2, "q_raw"), (3, "key_scales")):
-            pools.append(sb.tile([P, T], F32, name="val_pool%d" % b, tag=tag))
-            nc.sync.dma_start(pools[b][:], vals[b * P : (b + 1) * P, :])
-
-        scores = psum.tile([P, I], F32, name="scores")
-        nc.tensor.matmul_mx(
-            out=scores[:],
-            lhsT=q_codes[:].bitcast(FP8X4),
-            lhsT_scale=q_scales[:],
-            rhs=k_words[:].bitcast(FP4X4),
-            rhs_scale=k_scales[:],
-            start=True,
-            stop=True,
-        )
-
         os_bank = psum.tile([P, PACK, P], F32, name="os_bank")
         for t in range(PACK):
             nc.tensor.transpose(os_bank[:, t, :], os_cols[:, t : t + 1].to_broadcast([P, P]), ident[:])
+        os_rows = sb.tile([P, I], F32, name="os_rows")
+        nc.scalar.copy(out=os_rows[:].rearrange("q (s t) -> q s t", t=PACK), in_=os_bank[:].rearrange("q t s -> q s t"))
+
+        scores = []
+        for h in range(2):
+            half_list = slots[:, h * HALF // 16 : (h + 1) * HALF // 16]
+            k_words = sb.tile([P, HALF], U16, align_bytes=64, name="k_words%d" % h)
+            nc.vector.tensor_copy(k_words[:], key_words[:].indirect(half_list))
+            k_scales = sb.tile([P, HALF], U8, align_bytes=64, name="k_scales%d" % h, tag=("k_scales0", "q_grouped")[h])
+            nc.vector.tensor_copy(k_scales[:], key_scales[:].indirect(half_list))
+            scores.append(psum.tile([P, HALF], F32, name="scores%d" % h))
+            nc.tensor.matmul_mx(
+                out=scores[h][:],
+                lhsT=q_codes[:].bitcast(FP8X4),
+                lhsT_scale=q_scales[:],
+                rhs=k_words[:].bitcast(FP4X4),
+                rhs_scale=k_scales[:],
+                start=True,
+                stop=True,
+            )
 
         def gather_values(b, tag):
             picked = sb.tile([P, I], BF16, align_bytes=64, name="picked%d" % b, tag=tag)
             nc.vector.tensor_copy(picked[:], pools[b][:].indirect(slots[:]))
             return picked
 
-        neg_max = sb.tile([P, 1], F32, name="neg_max")
-        nc.vector.tensor_reduce(neg_max[:], scores[:], axis=mybir.AxisListType.X, op=ALU.max, negate=True)
+        neg_max0 = sb.tile([P, 1], F32, name="neg_max0")
+        nc.vector.tensor_reduce(neg_max0[:], scores[0][:], axis=mybir.AxisListType.X, op=ALU.max, negate=True)
+        neg_max = sb.tile([P, 1], F32, align_bytes=64, name="neg_max")
+        neg_scores = sb.tile([P, HALF], F32, align_bytes=64, name="neg_scores")
+        nc.vector.tensor_scalar(
+            neg_scores[:], scores[1][:], -1.0, neg_max0[:], ALU.mult, ALU.min, accum_out=neg_max[:]
+        )
+        z_parts = [sb.tile([P, 1], F32, name="z_part%d" % h) for h in range(2)]
+        for h in range(2):
+            nc.scalar.activation(
+                out=p[:, h * HALF : (h + 1) * HALF], in_=scores[h][:], func=ACT.Exp, bias=neg_max[:], accum_out=z_parts[h][:]
+            )
         shrink = sb.tile([P, 1], F32, name="shrink")
         nc.scalar.activation(out=shrink[:], in_=neg_max[:], func=ACT.Exp)
-        z = sb.tile([P, 1], F32, name="z")
-        nc.scalar.activation(out=p[:, :I], in_=scores[:], func=ACT.Exp, bias=neg_max[:], accum_out=z[:])
+        z_root = sb.tile([P, 1], F32, name="z_root")
+        nc.scalar.activation(out=z_root[:], in_=z_parts[0][:], func=ACT.Abs_reciprocal_sqrt, bias=z_parts[1][:])
         rest = sb.tile([P, 1], F32, name="rest")
         nc.scalar.activation(out=rest[:], in_=shrink[:], func=ACT.Identity, scale=reserve_col[:], bias=TINY)
-        z_root = sb.tile([P, 1], F32, name="z_root")
-        nc.scalar.activation(out=z_root[:], in_=z[:], func=ACT.Abs_reciprocal_sqrt)
         share = sb.tile([P, I], F32, align_bytes=64, name="share")
         nc.scalar.activation(out=share[:], in_=p[:, :I], func=ACT.Square, scale=z_root[:])
 
-        picked0 = gather_values(0, "k_words")
+        picked0 = gather_values(0, "neg_scores")
 
         linked = sb.tile([P, I], F32, align_bytes=64, name="linked")
         nc.vector.tensor_copy(linked[:], p[:].indirect(links[:]))
         pair = sb.tile([P, I], F32, name="pair")
-        nc.vector.tensor_tensor(pair[:], linked[:], p[:, :I], ALU.add)
-        root = sb.tile([P, I], F32, name="root")
+        nc.gpsimd.tensor_tensor(pair[:], linked[:], p[:, :I], ALU.add)
+        root = sb.tile([P, I], F32, align_bytes=64, name="root")
         nc.scalar.activation(out=root[:], in_=pair[:], func=ACT.Abs_reciprocal_sqrt, bias=rest[:])
         inv = sb.tile([P, I], F32, align_bytes=64, name="inv")
         nc.scalar.activation(out=inv[:], in_=root[:], func=ACT.Square)
-        picked1 = gather_values(1, "linked")
+        picked1 = gather_values(1, "neg_max")
         top = sb.tile([P, I], F32, name="top")
-        nc.vector.tensor_tensor(
-            top[:].rearrange("q (s t) -> q s t", t=PACK),
-            share[:].rearrange("q (s t) -> q s t", t=PACK),
-            os_bank[:].rearrange("q t s -> q s t"),
-            ALU.mult,
-        )
-        vq = [turn_and_quantise(nc, psum, sb, ident, picked0, "v0", "a")]
-        picked2 = gather_values(2, "share")
-        w = sb.tile([P, I], BF16, name="w")
+        nc.gpsimd.tensor_tensor(top[:], share[:], os_rows[:], ALU.mult)
+        picked2 = gather_values(2, "picked2")
+        w = sb.tile([P, I], BF16, align_bytes=64, name="w", tag="val_pool2")
         nc.vector.tensor_tensor(w[:], top[:], inv[:], ALU.mult)
         picked3 = gather_values(3, "inv")
-        vq.append(turn_and_quantise(nc, psum, sb, ident, picked1, "v1", "b"))
-        w_codes, w_scales = turn_and_quantise(nc, psum, sb, ident, w, "w", "w")
-        vq.append(turn_and_quantise(nc, psum, sb, ident, picked2, "v2", "a"))
-        vq.append(turn_and_quantise(nc, psum, sb, ident, picked3, "v3", "b"))
 
-        for b in range(BLOCKS):
-            acc = psum.tile([P, P], F32, name="acc%d" % (b % 2))
+        early = sb.tile([P, 2 * I], BF16, align_bytes=64, name="early", tag="root")
+        turn(nc, psum, ident, picked0, early[:, :I], "a")
+        turn(nc, psum, ident, picked1, early[:, I:], "b")
+        late = [sb.tile([P, I], BF16, align_bytes=64, name="late%d" % j) for j in range(3)]
+        turn(nc, psum, ident, picked2, late[0][:], "a")
+        turn(nc, psum, ident, w, late[1][:], "w")
+        turn(nc, psum, ident, picked3, late[2][:], "b")
+
+        codes = sb.tile([P, E + Q], U32, align_bytes=64, name="codes", tag="val_pool3")
+        scales = sb.tile([P, E + Q], U8, align_bytes=64, name="scales")
+        w_cols = slice(E, E + Q)
+        for cols, src in ((slice(0, 2 * P), early), (w_cols, late[1]), (slice(2 * P, 3 * P), late[0]), (slice(3 * P, E), late[2])):
+            nc.vector.quantize_mx(out=codes[:, cols].bitcast(FP8X4), scales=scales[:, cols], in_=src[:])
+
+        for j, cols in enumerate((slice(0, 2 * P), slice(2 * P, 3 * P), slice(3 * P, E))):
+            width = cols.stop - cols.start
+            acc = psum.tile([P, width], F32, name="acc%d" % (j % 2))
             nc.tensor.matmul_mx(
                 out=acc[:],
-                lhsT=w_codes[:].bitcast(FP8X4),
-                lhsT_scale=w_scales[:],
-                rhs=vq[b][0][:].bitcast(FP8X4),
-                rhs_scale=vq[b][1][:],
+                lhsT=codes[:, w_cols].bitcast(FP8X4),
+                lhsT_scale=scales[:, w_cols],
+                rhs=codes[:, cols].bitcast(FP8X4),
+                rhs_scale=scales[:, cols],
                 start=True,
                 stop=True,
             )
-            res = sb.tile([P, P], F32, name="res%d" % b)
+            res = sb.tile([P, width], F32, name="res%d" % j)
             nc.scalar.copy(out=res[:], in_=acc[:])
-            nc.sync.dma_start(out[:, b * P : (b + 1) * P], res[:])
+            nc.sync.dma_start(out[:, cols], res[:])

@@ -20,8 +20,7 @@ ALU = mybir.AluOpType
 P = 128
 PACK = 4
 BLOCKS = E // P
-P_WINDOW = 704
-CLEAR_SPLIT = 1408
+CLEAR_SPLIT = 1024
 HALF = I // 2
 TINY = 2.0 ** -100
 
@@ -72,8 +71,7 @@ def tile_attend_neighbourshare_kernel(tc, query, keys_words, keys_scales, reserv
         ident = sb.tile([P, P], F32, name="ident")
         make_identity(nc, ident[:])
 
-        p = sb.tile([P, P_WINDOW], F32, name="p")
-        nc.vector.memset(p[:, I:], 0.0)
+        p = sb.tile([P, I], F32, name="p")
 
         q_grouped = sb.tile([P, Q, PACK], BF16, align_bytes=64, name="q_grouped")
         nc.scalar.activation(out=q_grouped[:], in_=q_raw[:].rearrange("p j q -> p q j"), func=ACT.Copy)
@@ -126,30 +124,37 @@ def tile_attend_neighbourshare_kernel(tc, query, keys_words, keys_scales, reserv
             )
         shrink = sb.tile([P, 1], F32, name="shrink")
         nc.scalar.activation(out=shrink[:], in_=neg_max[:], func=ACT.Exp)
+        share = sb.tile([P, I], F32, align_bytes=64, name="share")
+        nc.scalar.activation(out=share[:], in_=p[:], func=ACT.Square)
         z_root = sb.tile([P, 1], F32, name="z_root")
         nc.scalar.activation(out=z_root[:], in_=z_parts[0][:], func=ACT.Abs_reciprocal_sqrt, bias=z_parts[1][:])
         rest = sb.tile([P, 1], F32, name="rest")
         nc.scalar.activation(out=rest[:], in_=shrink[:], func=ACT.Identity, scale=reserve_col[:], bias=TINY)
-        share = sb.tile([P, I], F32, align_bytes=64, name="share")
-        nc.scalar.activation(out=share[:], in_=p[:, :I], func=ACT.Square, scale=z_root[:])
 
         picked0 = gather_values(0, "neg_scores")
 
-        linked = sb.tile([P, I], F32, align_bytes=64, name="linked")
-        nc.vector.tensor_copy(linked[:], p[:].indirect(links[:]))
+        halves = [slice(h * HALF, (h + 1) * HALF) for h in range(2)]
         pair = sb.tile([P, I], F32, name="pair")
-        nc.gpsimd.tensor_tensor(pair[:], linked[:], p[:, :I], ALU.add)
+        for h, cols in enumerate(halves):
+            linked = sb.tile([P, HALF], F32, align_bytes=64, name="linked%d" % h)
+            nc.vector.tensor_copy(linked[:], p[:].indirect(links[:, h * HALF // 16 : (h + 1) * HALF // 16]))
+            nc.gpsimd.tensor_tensor(pair[:, cols], linked[:], p[:, cols], ALU.add)
         root = sb.tile([P, I], F32, align_bytes=64, name="root")
-        nc.scalar.activation(out=root[:], in_=pair[:], func=ACT.Abs_reciprocal_sqrt, bias=rest[:])
-        inv = sb.tile([P, I], F32, align_bytes=64, name="inv")
-        nc.scalar.activation(out=inv[:], in_=root[:], func=ACT.Square)
+        inv = sb.tile([P, I], F32, name="inv")
+        for cols in halves:
+            nc.scalar.activation(out=root[:, cols], in_=pair[:, cols], func=ACT.Abs_reciprocal_sqrt, bias=rest[:])
+        for cols in halves:
+            nc.scalar.activation(out=inv[:, cols], in_=root[:, cols], func=ACT.Square, scale=z_root[:])
         picked1 = gather_values(1, "neg_max")
-        top = sb.tile([P, I], F32, name="top")
-        nc.gpsimd.tensor_tensor(top[:], share[:], os_rows[:], ALU.mult)
+        tops = []
+        for h, cols in enumerate(halves):
+            tops.append(sb.tile([P, HALF], F32, align_bytes=64, name="top%d" % h, tag="linked%d" % h))
+            nc.gpsimd.tensor_tensor(tops[h][:], share[:, cols], os_rows[:, cols], ALU.mult)
         picked2 = gather_values(2, "picked2")
         w = sb.tile([P, I], BF16, align_bytes=64, name="w", tag="val_pool2")
-        nc.vector.tensor_tensor(w[:], top[:], inv[:], ALU.mult)
-        picked3 = gather_values(3, "inv")
+        for engine, top, cols in zip((nc.vector, nc.gpsimd), tops, halves):
+            engine.tensor_tensor(w[:, cols], top[:], inv[:, cols], ALU.mult)
+        picked3 = gather_values(3, "linked0")
 
         early = sb.tile([P, 2 * I], BF16, align_bytes=64, name="early", tag="root")
         turn(nc, psum, ident, picked0, early[:, :I], "a")
@@ -179,4 +184,4 @@ def tile_attend_neighbourshare_kernel(tc, query, keys_words, keys_scales, reserv
             )
             res = sb.tile([P, width], F32, name="res%d" % j)
             nc.scalar.copy(out=res[:], in_=acc[:])
-            nc.sync.dma_start(out[:, cols], res[:])
+            (nc.scalar if cols.stop == E else nc.sync).dma_start(out[:, cols], res[:])

from contextlib import ExitStack

import concourse.mybir as mybir
from concourse.masks import make_identity

D, E, T, I, Q = 512, 512, 2048, 512, 128
FLOPS = 2 * Q * I * D + 2 * Q * I * E

F32 = mybir.dt.float32
BF16 = mybir.dt.bfloat16
I32 = mybir.dt.int32
U32 = mybir.dt.uint32
U16 = mybir.dt.uint16
U8 = mybir.dt.uint8
FP8X4 = mybir.dt.float8_e4m3fn_x4
FP4X4 = mybir.dt.float4_e2m1fn_x4
ACT = mybir.ActivationFunctionType
ALU = mybir.AluOpType

P = 128
PACK = 4
BLOCKS = E // P
CLEAR_SPLIT = 1024
HALF = I // 2
TINY = 2.0 ** -100


def turn(nc, psum, ident, rows_bf16, grouped, bank):
    words = rows_bf16[:].bitcast(F32)
    turned = psum.tile([P, 2, P], F32, name="turned_" + bank)
    for u in range(2):
        nc.tensor.transpose(turned[:, u, :], words[:, u::2], ident[:])
    nc.scalar.copy(
        out=grouped.bitcast(F32).rearrange("s (c u) -> s c u", u=2),
        in_=turned[:].rearrange("s u c -> s c u"),
    )


def tile_attend_neighbourshare_kernel(tc, query, keys_words, keys_scales, reserve, slot_factor, vals, offs2, offs, out):
    nc = tc.nc
    with ExitStack() as ctx:
        sb = ctx.enter_context(tc.tile_pool(name="sb", bufs=1))
        psum = ctx.enter_context(tc.psum_pool(name="psum", bufs=1))

        key_scales = sb.tile([P, T], U8, name="key_scales")
        nc.vector.memset(key_scales[:, :CLEAR_SPLIT].bitcast(I32), 0)
        nc.gpsimd.memset(key_scales[:, CLEAR_SPLIT:].bitcast(I32), 0)

        slots = sb.tile([P, I // 16], U16, name="slots")
        nc.sync.dma_start(slots[:], offs)
        key_words = sb.tile([P, T], U16, name="key_words")
        nc.sync.dma_start(key_words[:].bitcast(I32), keys_words[0].bitcast(I32))
        for quad in range(4):
            nc.sync.dma_start(
                key_scales[32 * quad : 32 * quad + 4, :].bitcast(I32),
                keys_scales[0, 4 * quad : 4 * quad + 4, :].bitcast(I32),
            )
        q_raw = sb.tile([P, PACK, Q], F32, name="q_raw")
        nc.sync.dma_start(q_raw[:], query.rearrange("(p j) q -> p j q", j=PACK))
        os_cols = sb.tile([P, PACK], F32, name="os_cols")
        nc.sync.dma_start(os_cols[:], slot_factor.rearrange("o (s t) -> (o s) t", t=PACK))
        pools = [sb.tile([P, T], F32, align_bytes=64, name="val_pool%d" % b) for b in range(BLOCKS)]
        nc.sync.dma_start(pools[0][:], vals[0:P, :])
        links = sb.tile([P, I // 16], U16, name="links")
        nc.sync.dma_start(links[:], offs2)
        reserve_col = sb.tile([P, 1], F32, name="reserve_col")
        nc.sync.dma_start(reserve_col[:], reserve)
        for b in range(1, BLOCKS):
            nc.sync.dma_start(pools[b][:], vals[b * P : (b + 1) * P, :])

        ident = sb.tile([P, P], F32, name="ident")
        make_identity(nc, ident[:])

        p = sb.tile([P, I], F32, name="p")

        q_grouped = sb.tile([P, Q, PACK], BF16, align_bytes=64, name="q_grouped")
        nc.scalar.activation(out=q_grouped[:], in_=q_raw[:].rearrange("p j q -> p q j"), func=ACT.Copy)
        q_codes = sb.tile([P, Q], U32, align_bytes=64, name="q_codes")
        q_scales = sb.tile([P, Q], U8, align_bytes=64, name="q_scales")
        nc.vector.quantize_mx(
            out=q_codes[:].bitcast(FP8X4), scales=q_scales[:], in_=q_grouped[:].rearrange("p q j -> p (q j)")
        )

        os_bank = psum.tile([P, PACK, P], F32, name="os_bank")
        for t in range(PACK):
            nc.tensor.transpose(os_bank[:, t, :], os_cols[:, t : t + 1].to_broadcast([P, P]), ident[:])
        os_rows = sb.tile([P, I], F32, name="os_rows")
        nc.scalar.copy(out=os_rows[:].rearrange("q (s t) -> q s t", t=PACK), in_=os_bank[:].rearrange("q t s -> q s t"))

        scores = []
        for h in range(2):
            half_list = slots[:, h * HALF // 16 : (h + 1) * HALF // 16]
            k_words = sb.tile([P, HALF], U16, align_bytes=64, name="k_words%d" % h)
            nc.vector.tensor_copy(k_words[:], key_words[:].indirect(half_list))
            k_scales = sb.tile([P, HALF], U8, align_bytes=64, name="k_scales%d" % h, tag=("k_scales0", "q_grouped")[h])
            nc.vector.tensor_copy(k_scales[:], key_scales[:].indirect(half_list))
            scores.append(psum.tile([P, HALF], F32, name="scores%d" % h))
            nc.tensor.matmul_mx(
                out=scores[h][:],
                lhsT=q_codes[:].bitcast(FP8X4),
                lhsT_scale=q_scales[:],
                rhs=k_words[:].bitcast(FP4X4),
                rhs_scale=k_scales[:],
                start=True,
                stop=True,
            )

        def gather_values(b, tag):
            picked = sb.tile([P, I], BF16, align_bytes=64, name="picked%d" % b, tag=tag)
            nc.vector.tensor_copy(picked[:], pools[b][:].indirect(slots[:]))
            return picked

        neg_max0 = sb.tile([P, 1], F32, name="neg_max0")
        nc.vector.tensor_reduce(neg_max0[:], scores[0][:], axis=mybir.AxisListType.X, op=ALU.max, negate=True)
        neg_max = sb.tile([P, 1], F32, align_bytes=64, name="neg_max")
        neg_scores = sb.tile([P, HALF], F32, align_bytes=64, name="neg_scores")
        nc.vector.tensor_scalar(
            neg_scores[:], scores[1][:], -1.0, neg_max0[:], ALU.mult, ALU.min, accum_out=neg_max[:]
        )
        z_parts = [sb.tile([P, 1], F32, name="z_part%d" % h) for h in range(2)]
        for h in range(2):
            nc.scalar.activation(
                out=p[:, h * HALF : (h + 1) * HALF], in_=scores[h][:], func=ACT.Exp, bias=neg_max[:], accum_out=z_parts[h][:]
            )
        shrink = sb.tile([P, 1], F32, name="shrink")
        nc.scalar.activation(out=shrink[:], in_=neg_max[:], func=ACT.Exp)
        share = sb.tile([P, I], F32, align_bytes=64, name="share")
        nc.scalar.activation(out=share[:], in_=p[:], func=ACT.Square)
        z_root = sb.tile([P, 1], F32, name="z_root")
        nc.scalar.activation(out=z_root[:], in_=z_parts[0][:], func=ACT.Abs_reciprocal_sqrt, bias=z_parts[1][:])
        rest = sb.tile([P, 1], F32, name="rest")
        nc.scalar.activation(out=rest[:], in_=shrink[:], func=ACT.Identity, scale=reserve_col[:], bias=TINY)

        picked0 = gather_values(0, "neg_scores")

        halves = [slice(h * HALF, (h + 1) * HALF) for h in range(2)]
        pair = sb.tile([P, I], F32, name="pair")
        for h, cols in enumerate(halves):
            linked = sb.tile([P, HALF], F32, align_bytes=64, name="linked%d" % h)
            nc.vector.tensor_copy(linked[:], p[:].indirect(links[:, h * HALF // 16 : (h + 1) * HALF // 16]))
            nc.gpsimd.tensor_tensor(pair[:, cols], linked[:], p[:, cols], ALU.add)
        root = sb.tile([P, I], F32, align_bytes=64, name="root")
        inv = sb.tile([P, I], F32, name="inv")
        for cols in halves:
            nc.scalar.activation(out=root[:, cols], in_=pair[:, cols], func=ACT.Abs_reciprocal_sqrt, bias=rest[:])
        for cols in halves:
            nc.scalar.activation(out=inv[:, cols], in_=root[:, cols], func=ACT.Square, scale=z_root[:])
        picked1 = gather_values(1, "neg_max")
        tops = []
        for h, cols in enumerate(halves):
            tops.append(sb.tile([P, HALF], F32, align_bytes=64, name="top%d" % h, tag="linked%d" % h))
            nc.gpsimd.tensor_tensor(tops[h][:], share[:, cols], os_rows[:, cols], ALU.mult)
        picked2 = gather_values(2, "picked2")
        w = sb.tile([P, I], BF16, align_bytes=64, name="w", tag="val_pool2")
        for engine, top, cols in zip((nc.vector, nc.gpsimd), tops, halves):
            engine.tensor_tensor(w[:, cols], top[:], inv[:, cols], ALU.mult)
        picked3 = gather_values(3, "linked0")

        early = sb.tile([P, 2 * I], BF16, align_bytes=64, name="early", tag="root")
        turn(nc, psum, ident, picked0, early[:, :I], "a")
        turn(nc, psum, ident, picked1, early[:, I:], "b")
        late = [sb.tile([P, I], BF16, align_bytes=64, name="late%d" % j) for j in range(3)]
        turn(nc, psum, ident, picked2, late[0][:], "a")
        turn(nc, psum, ident, w, late[1][:], "w")
        turn(nc, psum, ident, picked3, late[2][:], "b")

        codes = sb.tile([P, E + Q], U32, align_bytes=64, name="codes", tag="val_pool3")
        scales = sb.tile([P, E + Q], U8, align_bytes=64, name="scales")
        w_cols = slice(E, E + Q)
        for cols, src in ((slice(0, 2 * P), early), (w_cols, late[1]), (slice(2 * P, 3 * P), late[0]), (slice(3 * P, E), late[2])):
            nc.vector.quantize_mx(out=codes[:, cols].bitcast(FP8X4), scales=scales[:, cols], in_=src[:])

        for j, cols in enumerate((slice(0, 2 * P), slice(2 * P, 3 * P), slice(3 * P, E))):
            width = cols.stop - cols.start
            acc = psum.tile([P, width], F32, name="acc%d" % (j % 2))
            nc.tensor.matmul_mx(
                out=acc[:],
                lhsT=codes[:, w_cols].bitcast(FP8X4),
                lhsT_scale=scales[:, w_cols],
                rhs=codes[:, cols].bitcast(FP8X4),
                rhs_scale=scales[:, cols],
                start=True,
                stop=True,
            )
            res = sb.tile([P, width], F32, name="res%d" % j)
            nc.scalar.copy(out=res[:], in_=acc[:])
            (nc.scalar if cols.stop == E else nc.sync).dma_start(out[:, cols], res[:])
